import numpy as np
import ml_dtypes


def mxq(x, axis, fmt="e4m3"):
    dtype, down = {"e4m3": (ml_dtypes.float8_e4m3fn, 7), "e5m2": (ml_dtypes.float8_e5m2, 14)}[fmt]
    v = np.moveaxis(np.asarray(x, np.float32).astype(ml_dtypes.bfloat16).astype(np.float64), axis, -1)
    blocks = v.reshape(v.shape[:-1] + (-1, 32))
    amax = np.abs(blocks).max(-1, keepdims=True)
    byte = np.maximum(np.where(amax > 0, np.frexp(amax)[1] - 1 + 127, 0) - down, 1)
    scale = np.exp2(byte - 127.0)
    codes = (blocks / scale).astype(np.float32).astype(dtype).astype(np.float64)
    return np.moveaxis((codes * scale).reshape(v.shape), -1, axis)


WIDE = False


def mx_kscale(k):
    if not WIDE:
        return np.ones(k)
    levels = np.array([10, -10, 5, -5, 0])
    if k % 512:
        return np.exp2(np.random.permutation(np.resize(levels, k // 32))).repeat(32)
    a = np.empty((k // 512, 16))
    for p in range(k // 512):
        a[p, :8] = np.random.permutation(np.resize(levels, 8))
        for g in range(8):
            far = levels[np.abs(levels - a[p, g]) >= 10]
            a[p, g + 8] = far[np.random.randint(len(far))]
    return np.exp2(a.ravel()).repeat(32)


def f64(x):
    return np.asarray(x).astype(np.float64)


def striped(idx):
    return np.tile(idx.reshape(-1, 16).T, (8, 1)).astype(np.uint16)


def unstriped(offs):
    return offs[:16].T.reshape(-1).astype(np.int64)


def pack_weight(w):
    k, n = w.shape
    w = f64(np.asarray(w, np.float32).astype(ml_dtypes.bfloat16)).reshape(k // 32, 32, n)
    amax = np.abs(w).max(1)
    byte = np.clip(np.where(amax > 0, np.frexp(amax)[1] - 1 + 127 - 7, 1), 1, 254)
    scaled = (w * np.exp2(127.0 - byte)[:, None, :]).reshape(k, n).astype(np.float32)
    words = np.ascontiguousarray(scaled.reshape(k // 512, 128, 4, n).transpose(0, 1, 3, 2)).astype(ml_dtypes.float8_e4m3fn).view(np.uint8)
    return words, np.ascontiguousarray(byte.astype(np.uint8).reshape(k // 512, 16, n))


def unpack_weight(words, scales):
    g, p, n, _ = words.shape
    vals = np.ascontiguousarray(words).view(ml_dtypes.float8_e4m3fn).astype(np.float64) * np.repeat(np.exp2(scales.astype(np.float64) - 127.0), 8, axis=1)[..., None]
    return vals.transpose(0, 1, 3, 2).reshape(g * 512, n)

def planes(y):
    n, m = y.shape
    v = y.astype(np.float32).astype(ml_dtypes.bfloat16).astype(np.float64).reshape(n // 32, 32, m)
    top = np.abs(v).max(1)
    byte = np.clip(np.where(top > 0, np.frexp(top)[1] - 1 + 127 - 7, 1), 1, 254)
    codes = (v * np.exp2(127.0 - byte)[:, None, :]).reshape(n, m).astype(np.float32).astype(ml_dtypes.float8_e4m3fn).view(np.uint8)
    words = codes.reshape(n // 512, 128, 4, m).transpose(0, 1, 3, 2)
    return np.ascontiguousarray(words), np.ascontiguousarray(byte.astype(np.uint8).reshape(n // 512, 16, m))


K, T, S, N = 512, 1024, 512, 512


def setup_inputs():
    n = np.random.standard_normal
    s = mx_kscale(K)[:, None]
    packed_xT = pack_weight(n((K, T)) * s)
    return {
        "x_words": packed_xT[0],
        "x_scales": packed_xT[1],
        "w1": (n((K, N)) / np.sqrt(K) / s).astype(np.float32),
        "w2": (n((K, N)) / np.sqrt(K) / s).astype(np.float32),
        "w3": (n((K, N)) / np.sqrt(K) / s).astype(np.float32),
        "offs": striped(np.random.permutation(T)[:S]),
    }


def reference(x_words, x_scales, w1, w2, w3, offs):
    xq = unpack_weight(x_words, x_scales)[:, unstriped(offs)]
    out_0 = np.maximum(np.maximum(mxq(f64(w1), 0, "e4m3").T @ xq, mxq(f64(w2), 0, "e4m3").T @ xq), mxq(f64(w3), 0, "e4m3").T @ xq)
    return (out_0,) + planes(out_0)

@@ -1,0 +1,163 @@
+from contextlib import ExitStack
+
+import concourse.mybir as mybir
+
+K, T, S, N = 512, 1024, 512, 512
+FLOPS = 3 * 2 * K * S * N
+
+F32 = mybir.dt.float32
+BF16 = mybir.dt.bfloat16
+I32 = mybir.dt.int32
+U32 = mybir.dt.uint32
+U16 = mybir.dt.uint16
+U8 = mybir.dt.uint8
+FP8X4 = mybir.dt.float8_e4m3fn_x4
+MAX = mybir.AluOpType.max
+
+P = 128
+PACK = 4
+HALF = 256
+
+
+def tile_picked_maxout_max_po_kernel(
+    tc, x_words, x_scales, w1, w2, w3, offs, out_0, out_1, out_2
+):
+    nc = tc.nc
+    with ExitStack() as ctx:
+        sb = ctx.enter_context(tc.tile_pool(name="sb", bufs=1))
+        psum = ctx.enter_context(tc.psum_pool(name="psum", bufs=1))
+
+        def sbuf(name, shape, dtype):
+            return sb.tile(shape, dtype, name=name, align_bytes=64)
+
+        offsets = sb.tile([P, S // 16], U16, name="offsets")
+        nc.sync.dma_start(offsets[:], offs)
+
+        scale_table = sbuf("scale_table", [P, T], U8)
+        nc.vector.memset(scale_table[:].bitcast(I32), 0)
+        for q in range(4):
+            nc.scalar.dma_start(
+                scale_table[32 * q : 32 * q + 4, :].bitcast(I32),
+                x_scales[0, 4 * q : 4 * q + 4, :].bitcast(I32),
+            )
+
+        word_table = sbuf("word_table", [P, T], I32)
+        nc.sync.dma_start(word_table[:], x_words[0].rearrange("p n t -> p (n t)").bitcast(I32))
+
+        raw = {}
+        for i, w in enumerate((w1, w2, w3)):
+            rows = w.rearrange("(p j) c -> p j c", j=PACK)
+            for h in range(2):
+                raw[i, h] = sbuf("raw%d_%d" % (i, h), [P, PACK, HALF], F32)
+                nc.sync.dma_start(raw[i, h][:], rows[:, :, h * HALF : (h + 1) * HALF])
+
+        x_scale = sbuf("x_scale", [P, S], U8)
+        x_code = sbuf("x_code", [P, S], U32)
+        nc.vector.tensor_copy(x_scale[:], scale_table[:].indirect(offsets[:]))
+        nc.vector.tensor_copy(x_code[:], word_table[:].bitcast(U32).indirect(offsets[:]))
+
+        grouped = [sbuf("grouped%d" % i, [P, PACK, P, PACK], BF16) for i in range(3)]
+        w_code = {}
+        w_scale = {}
+
+        def cast(copy, i, h):
+            copy(
+                grouped[i][:, :, 64 * h : 64 * h + 64, :].rearrange("p t m j -> p m j t"),
+                raw[i, h][:].rearrange("p j (m t) -> p m j t", t=PACK),
+            )
+
+        def quantize(i, u):
+            w_code[i, u] = sbuf("w_code%d_%d" % (i, u), [P, 2 * P], U32)
+            w_scale[i, u] = sbuf("w_scale%d_%d" % (i, u), [P, 2 * P], U8)
+            nc.vector.quantize_mx(
+                out=w_code[i, u][:].bitcast(FP8X4),
+                scales=w_scale[i, u][:],
+                in_=grouped[i][:, 2 * u : 2 * u + 2, :, :].rearrange("p t m j -> p (t m j)"),
+            )
+
+        def product(i, u, h, bank):
+            acc = psum.tile([P, 2, HALF], F32, name="acc%d_%d_%d" % (i, u, h), tag="bank%d" % bank)
+            cols = slice(h * HALF, (h + 1) * HALF)
+            for e in range(2):
+                rows_e = slice(e * P, (e + 1) * P)
+                nc.tensor.matmul_mx(
+                    out=acc[:, e, :],
+                    lhsT=w_code[i, u][:, rows_e].bitcast(FP8X4),
+                    lhsT_scale=w_scale[i, u][:, rows_e],
+                    rhs=x_code[:, cols].bitcast(FP8X4),
+                    rhs_scale=x_scale[:, cols],
+                    start=True,
+                    stop=True,
+                )
+            return acc
+
+        by_pair = [(u, h) for u in range(2) for h in range(2)]
+        by_half = [(u, h) for h in range(2) for u in range(2)]
+
+        cast(nc.scalar.copy, 0, 0)
+        cast(nc.vector.tensor_copy, 0, 1)
+        quantize(0, 0)
+        quantize(0, 1)
+        first = {}
+        for u, h in by_pair:
+            acc = product(0, u, h, 2 * u + h)
+            first[u, h] = sbuf("first%d_%d" % (u, h), [P, 2, HALF], F32)
+            nc.scalar.copy(first[u, h][:], acc[:])
+
+        cast(nc.vector.tensor_copy, 1, 0)
+        cast(nc.vector.tensor_copy, 1, 1)
+        quantize(1, 0)
+        quantize(1, 1)
+        cast(nc.scalar.copy, 2, 0)
+        cast(nc.scalar.copy, 2, 1)
+        second = {}
+        for u, h in by_pair:
+            acc = product(1, u, h, 4 + 2 * u + h)
+            second[u, h] = sbuf("second%d_%d" % (u, h), [P, 2, HALF], F32)
+            nc.vector.tensor_tensor(second[u, h][:], acc[:], first[u, h][:], MAX)
+
+        quantize(2, 0)
+        quantize(2, 1)
+        y = [sbuf("y%d" % h, [P, PACK, HALF], F32) for h in range(2)]
+        y_rows = out_0.rearrange("(p t) n -> p t n", t=PACK)
+        y_code = sbuf("y_code", [P, S], U32)
+        y_scale = sbuf("y_scale", [P, S], U8)
+        code_rows = out_1[0].rearrange("p n t -> p (n t)").bitcast(I32)
+
+        def round_y(copy, name, h, c0, c1):
+            g = sbuf(name, [P, c1 - c0, PACK], BF16)
+            copy(
+                g[:].rearrange("p (c i) t -> p c t i", i=4),
+                y[h][:, :, c0:c1].rearrange("p t (c i) -> p c t i", i=4),
+            )
+            return g
+
+        def quantize_y(g, c0, c1):
+            nc.vector.quantize_mx(
+                out=y_code[:, c0:c1].bitcast(FP8X4),
+                scales=y_scale[:, c0:c1],
+                in_=g[:].rearrange("p n t -> p (n t)"),
+            )
+
+        for u, h in by_half:
+            acc = product(2, u, h, 2 * u + h)
+            nc.vector.tensor_tensor(y[h][:, 2 * u : 2 * u + 2, :], acc[:], second[u, h][:], MAX)
+            nc.sync.dma_start(
+                y_rows[:, 2 * u : 2 * u + 2, h * HALF : (h + 1) * HALF], y[h][:, 2 * u : 2 * u + 2, :]
+            )
+            if (u, h) == (1, 0):
+                g0 = round_y(nc.scalar.copy, "y_round0", 0, 0, HALF)
+
+        g2 = round_y(nc.scalar.copy, "y_round2", 1, P, HALF)
+        quantize_y(g0, 0, HALF)
+        nc.sync.dma_start(code_rows[:, 0:HALF], y_code[:, 0:HALF].bitcast(I32))
+        g1 = round_y(nc.vector.tensor_copy, "y_round1", 1, 0, P)
+        quantize_y(g2, HALF + P, S)
+        quantize_y(g1, HALF, HALF + P)
+        nc.sync.dma_start(code_rows[:, HALF:S], y_code[:, HALF:S].bitcast(I32))
+        for q in range(4):
+            queue = nc.scalar if q < 2 else nc.sync
+            queue.dma_start(
+                out_2[0, 4 * q : 4 * q + 4, :].bitcast(I32),
+                y_scale[32 * q : 32 * q + 4, :].bitcast(I32),
+            )

@@ -35,14 +35,13 @@ def tile_picked_maxout_max_po_kernel(
 
         scale_table = sbuf("scale_table", [P, T], U8)
         nc.vector.memset(scale_table[:].bitcast(I32), 0)
+        word_table = sbuf("word_table", [P, T], I32)
+        nc.sync.dma_start(word_table[:], x_words[0].rearrange("p n t -> p (n t)").bitcast(I32))
         for q in range(4):
-            nc.scalar.dma_start(
+            nc.sync.dma_start(
                 scale_table[32 * q : 32 * q + 4, :].bitcast(I32),
                 x_scales[0, 4 * q : 4 * q + 4, :].bitcast(I32),
             )
-
-        word_table = sbuf("word_table", [P, T], I32)
-        nc.sync.dma_start(word_table[:], x_words[0].rearrange("p n t -> p (n t)").bitcast(I32))
 
         raw = {}
         for i, w in enumerate((w1, w2, w3)):
@@ -53,18 +52,23 @@ def tile_picked_maxout_max_po_kernel(
 
         x_scale = sbuf("x_scale", [P, S], U8)
         x_code = sbuf("x_code", [P, S], U32)
-        nc.vector.tensor_copy(x_scale[:], scale_table[:].indirect(offsets[:]))
         nc.vector.tensor_copy(x_code[:], word_table[:].bitcast(U32).indirect(offsets[:]))
+        nc.vector.tensor_copy(x_scale[:], scale_table[:].indirect(offsets[:]))
 
-        grouped = [sbuf("grouped%d" % i, [P, PACK, P, PACK], BF16) for i in range(3)]
+        grouped = {}
         w_code = {}
         w_scale = {}
 
-        def cast(copy, i, h):
-            copy(
-                grouped[i][:, :, 64 * h : 64 * h + 64, :].rearrange("p t m j -> p m j t"),
-                raw[i, h][:].rearrange("p j (m t) -> p m j t", t=PACK),
-            )
+        def cast(copy, i, h, pairs):
+            for u in pairs:
+                if h == 0:
+                    grouped[i, u] = sb.tile(
+                        [P, 2, P, PACK], BF16, name="grouped%d_%d" % (i, u), tag="pair%d" % u, align_bytes=64
+                    )
+                copy(
+                    grouped[i, u][:, :, 64 * h : 64 * h + 64, :].rearrange("p t m j -> p m j t"),
+                    raw[i, h][:].rearrange("p j (m t) -> p m j t", t=PACK)[:, :, :, 2 * u : 2 * u + 2],
+                )
 
         def quantize(i, u):
             w_code[i, u] = sbuf("w_code%d_%d" % (i, u), [P, 2 * P], U32)
@@ -72,7 +76,7 @@ def tile_picked_maxout_max_po_kernel(
             nc.vector.quantize_mx(
                 out=w_code[i, u][:].bitcast(FP8X4),
                 scales=w_scale[i, u][:],
-                in_=grouped[i][:, 2 * u : 2 * u + 2, :, :].rearrange("p t m j -> p (t m j)"),
+                in_=grouped[i, u][:].rearrange("p t m j -> p (t m j)"),
             )
 
         def product(i, u, h, bank):
@@ -94,8 +98,8 @@ def tile_picked_maxout_max_po_kernel(
         by_pair = [(u, h) for u in range(2) for h in range(2)]
         by_half = [(u, h) for h in range(2) for u in range(2)]
 
-        cast(nc.scalar.copy, 0, 0)
-        cast(nc.vector.tensor_copy, 0, 1)
+        cast(nc.scalar.copy, 0, 0, (0, 1))
+        cast(nc.vector.tensor_copy, 0, 1, (0, 1))
         quantize(0, 0)
         quantize(0, 1)
         first = {}
@@ -104,20 +108,23 @@ def tile_picked_maxout_max_po_kernel(
             first[u, h] = sbuf("first%d_%d" % (u, h), [P, 2, HALF], F32)
             nc.scalar.copy(first[u, h][:], acc[:])
 
-        cast(nc.vector.tensor_copy, 1, 0)
-        cast(nc.vector.tensor_copy, 1, 1)
+        cast(nc.vector.tensor_copy, 1, 0, (0, 1))
+        cast(nc.vector.tensor_copy, 1, 1, (0, 1))
         quantize(1, 0)
         quantize(1, 1)
-        cast(nc.scalar.copy, 2, 0)
-        cast(nc.scalar.copy, 2, 1)
+        cast(nc.vector.tensor_copy, 2, 0, (0, 1))
+        cast(nc.scalar.copy, 2, 1, (0, 1))
         second = {}
         for u, h in by_pair:
             acc = product(1, u, h, 4 + 2 * u + h)
-            second[u, h] = sbuf("second%d_%d" % (u, h), [P, 2, HALF], F32)
+            if (u, h) == (1, 1):
+                quantize(2, 0)
+                quantize(2, 1)
+                second[u, h] = sb.tile([P, 2, HALF], F32, name="second_last", tag="pair1", align_bytes=64)
+            else:
+                second[u, h] = sbuf("second%d_%d" % (u, h), [P, 2, HALF], F32)
             nc.vector.tensor_tensor(second[u, h][:], acc[:], first[u, h][:], MAX)
 
-        quantize(2, 0)
-        quantize(2, 1)
         y = [sbuf("y%d" % h, [P, PACK, HALF], F32) for h in range(2)]
         y_rows = out_0.rearrange("(p t) n -> p t n", t=PACK)
         y_code = sbuf("y_code", [P, S], U32)
@@ -149,11 +156,11 @@ def tile_picked_maxout_max_po_kernel(
                 g0 = round_y(nc.scalar.copy, "y_round0", 0, 0, HALF)
 
         g2 = round_y(nc.scalar.copy, "y_round2", 1, P, HALF)
+        g1 = round_y(nc.vector.tensor_copy, "y_round1", 1, 0, P)
         quantize_y(g0, 0, HALF)
         nc.sync.dma_start(code_rows[:, 0:HALF], y_code[:, 0:HALF].bitcast(I32))
-        g1 = round_y(nc.vector.tensor_copy, "y_round1", 1, 0, P)
-        quantize_y(g2, HALF + P, S)
         quantize_y(g1, HALF, HALF + P)
+        quantize_y(g2, HALF + P, S)
         nc.sync.dma_start(code_rows[:, HALF:S], y_code[:, HALF:S].bitcast(I32))
         for q in range(4):
             queue = nc.scalar if q < 2 else nc.sync

@@ -39,8 +39,8 @@ def tile_picked_maxout_max_po_kernel(
         nc.sync.dma_start(word_table[:], x_words[0].rearrange("p n t -> p (n t)").bitcast(I32))
         for q in range(4):
             nc.sync.dma_start(
-                scale_table[32 * q : 32 * q + 4, :].bitcast(I32),
-                x_scales[0, 4 * q : 4 * q + 4, :].bitcast(I32),
+                scale_table[q:P:32, :].bitcast(I32),
+                x_scales[0, q:16:4, :].bitcast(I32),
             )
 
         raw = {}
@@ -112,7 +112,8 @@ def tile_picked_maxout_max_po_kernel(
         cast(nc.vector.tensor_copy, 1, 1, (0, 1))
         quantize(1, 0)
         quantize(1, 1)
-        cast(nc.vector.tensor_copy, 2, 0, (0, 1))
+        cast(nc.vector.tensor_copy, 2, 0, (0,))
+        cast(nc.scalar.copy, 2, 0, (1,))
         cast(nc.scalar.copy, 2, 1, (0, 1))
         second = {}
         for u, h in by_pair:
@@ -165,6 +166,6 @@ def tile_picked_maxout_max_po_kernel(
         for q in range(4):
             queue = nc.scalar if q < 2 else nc.sync
             queue.dma_start(
-                out_2[0, 4 * q : 4 * q + 4, :].bitcast(I32),
-                y_scale[32 * q : 32 * q + 4, :].bitcast(I32),
+                out_2[0, q:16:4, :].bitcast(I32),
+                y_scale[q:P:32, :].bitcast(I32),
             )

@@ -47,7 +47,7 @@ def tile_picked_maxout_max_po_kernel(
         for i, w in enumerate((w1, w2, w3)):
             rows = w.rearrange("(p j) c -> p j c", j=PACK)
             for h in range(2):
-                raw[i, h] = sbuf("raw%d_%d" % (i, h), [P, PACK, HALF], F32)
+                raw[i, h] = sb.tile([P, PACK, HALF], F32, name="raw%d_%d" % (i, h), tag="raw%d_%d" % (i, h), align_bytes=64)
                 nc.sync.dma_start(raw[i, h][:], rows[:, :, h * HALF : (h + 1) * HALF])
 
         x_scale = sbuf("x_scale", [P, S], U8)
@@ -113,15 +113,16 @@ def tile_picked_maxout_max_po_kernel(
         quantize(1, 0)
         quantize(1, 1)
         cast(nc.vector.tensor_copy, 2, 0, (0,))
+        cast(nc.scalar.copy, 2, 1, (0,))
         cast(nc.scalar.copy, 2, 0, (1,))
-        cast(nc.scalar.copy, 2, 1, (0, 1))
+        cast(nc.scalar.copy, 2, 1, (1,))
+        quantize(2, 0)
+        quantize(2, 1)
         second = {}
         for u, h in by_pair:
             acc = product(1, u, h, 4 + 2 * u + h)
             if (u, h) == (1, 1):
-                quantize(2, 0)
-                quantize(2, 1)
-                second[u, h] = sb.tile([P, 2, HALF], F32, name="second_last", tag="pair1", align_bytes=64)
+                second[u, h] = sb.tile([P, 2, HALF], F32, name="second_last", tag="raw2_1", align_bytes=64)
             else:
                 second[u, h] = sbuf("second%d_%d" % (u, h), [P, 2, HALF], F32)
             nc.vector.tensor_tensor(second[u, h][:], acc[:], first[u, h][:], MAX)

@@ -31,14 +31,15 @@ def tile_picked_maxout_max_po_kernel(
             return sb.tile(shape, dtype, name=name, align_bytes=64)
 
         offsets = sb.tile([P, S // 16], U16, name="offsets")
-        nc.sync.dma_start(offsets[:], offs)
 
         scale_table = sbuf("scale_table", [P, T], U8)
         nc.vector.memset(scale_table[:].bitcast(I32), 0)
         word_table = sbuf("word_table", [P, T], I32)
         nc.sync.dma_start(word_table[:], x_words[0].rearrange("p n t -> p (n t)").bitcast(I32))
+        nc.sync.dma_start(offsets[:], offs)
         for q in range(4):
-            nc.sync.dma_start(
+            queue = nc.scalar if q < 2 else nc.sync
+            queue.dma_start(
                 scale_table[q:P:32, :].bitcast(I32),
                 x_scales[0, q:16:4, :].bitcast(I32),
             )

@@ -13,6 +13,8 @@ U16 = mybir.dt.uint16
 U8 = mybir.dt.uint8
 FP8X4 = mybir.dt.float8_e4m3fn_x4
 MAX = mybir.AluOpType.max
+MULT = mybir.AluOpType.mult
+ADD = mybir.AluOpType.add
 
 P = 128
 PACK = 4
@@ -27,8 +29,8 @@ def tile_picked_maxout_max_po_kernel(
         sb = ctx.enter_context(tc.tile_pool(name="sb", bufs=1))
         psum = ctx.enter_context(tc.psum_pool(name="psum", bufs=1))
 
-        def sbuf(name, shape, dtype):
-            return sb.tile(shape, dtype, name=name, align_bytes=64)
+        def sbuf(name, shape, dtype, tag=None):
+            return sb.tile(shape, dtype, name=name, tag=tag or name, align_bytes=64)
 
         offsets = sb.tile([P, S // 16], U16, name="offsets")
 
@@ -56,6 +58,17 @@ def tile_picked_maxout_max_po_kernel(
         nc.vector.tensor_copy(x_code[:], word_table[:].bitcast(U32).indirect(offsets[:]))
         nc.vector.tensor_copy(x_scale[:], scale_table[:].indirect(offsets[:]))
 
+        warm = psum.tile([P, S], F32, name="warm", tag="bank7")
+        nc.tensor.matmul_mx(
+            out=warm[:],
+            lhsT=x_code[:, 0:P].bitcast(FP8X4),
+            lhsT_scale=x_scale[:, 0:P],
+            rhs=x_code[:].bitcast(FP8X4),
+            rhs_scale=x_scale[:],
+            start=True,
+            stop=True,
+        )
+
         grouped = {}
         w_code = {}
         w_scale = {}
@@ -63,9 +76,7 @@ def tile_picked_maxout_max_po_kernel(
         def cast(copy, i, h, pairs):
             for u in pairs:
                 if h == 0:
-                    grouped[i, u] = sb.tile(
-                        [P, 2, P, PACK], BF16, name="grouped%d_%d" % (i, u), tag="pair%d" % u, align_bytes=64
-                    )
+                    grouped[i, u] = sbuf("grouped%d_%d" % (i, u), [P, 2, P, PACK], BF16, tag="pair%d" % u)
                 copy(
                     grouped[i, u][:, :, 64 * h : 64 * h + 64, :].rearrange("p t m j -> p m j t"),
                     raw[i, h][:].rearrange("p j (m t) -> p m j t", t=PACK)[:, :, :, 2 * u : 2 * u + 2],
@@ -114,19 +125,29 @@ def tile_picked_maxout_max_po_kernel(
         quantize(1, 0)
         quantize(1, 1)
         cast(nc.vector.tensor_copy, 2, 0, (0,))
-        cast(nc.scalar.copy, 2, 1, (0,))
-        cast(nc.scalar.copy, 2, 0, (1,))
-        cast(nc.scalar.copy, 2, 1, (1,))
+        second = {}
+
+        def second_max(u, h, tag=None):
+            acc = product(1, u, h, 5 if (u, h) == (1, 1) else 4 + 2 * u + h)
+            second[u, h] = sbuf("second%d_%d" % (u, h), [P, 2, HALF], F32, tag=tag)
+            nc.vector.tensor_tensor(second[u, h][:], acc[:], first[u, h][:], MAX)
+
+        second_max(0, 0)
+        grouped[2, 1] = sbuf("grouped2_1", [P, 2, P, PACK], BF16, tag="first0_0")
+        nc.gpsimd.tensor_scalar(
+            grouped[2, 1][:, :, 0:64, :].rearrange("p t m j -> p m t j"),
+            raw[2, 0][:].rearrange("p j (m t) -> p m t j", t=PACK)[:, :, 2:4, :],
+            1.0,
+            0.0,
+            MULT,
+            ADD,
+        )
+        cast(nc.scalar.copy, 2, 1, (0, 1))
         quantize(2, 0)
         quantize(2, 1)
-        second = {}
-        for u, h in by_pair:
-            acc = product(1, u, h, 4 + 2 * u + h)
-            if (u, h) == (1, 1):
-                second[u, h] = sb.tile([P, 2, HALF], F32, name="second_last", tag="raw2_1", align_bytes=64)
-            else:
-                second[u, h] = sbuf("second%d_%d" % (u, h), [P, 2, HALF], F32)
-            nc.vector.tensor_tensor(second[u, h][:], acc[:], first[u, h][:], MAX)
+        second_max(0, 1)
+        second_max(1, 0)
+        second_max(1, 1, tag="raw2_1")
 
         y = [sbuf("y%d" % h, [P, PACK, HALF], F32) for h in range(2)]
         y_rows = out_0.rearrange("(p t) n -> p t n", t=PACK)

@@ -46,12 +46,14 @@ def tile_picked_maxout_max_po_kernel(
                 x_scales[0, q:16:4, :].bitcast(I32),
             )
 
+        pieces = ((0, 256, 512), (0, 256, 512), (0, 256, 384, 512))
         raw = {}
         for i, w in enumerate((w1, w2, w3)):
             rows = w.rearrange("(p j) c -> p j c", j=PACK)
-            for h in range(2):
-                raw[i, h] = sb.tile([P, PACK, HALF], F32, name="raw%d_%d" % (i, h), tag="raw%d_%d" % (i, h), align_bytes=64)
-                nc.sync.dma_start(raw[i, h][:], rows[:, :, h * HALF : (h + 1) * HALF])
+            for h in range(len(pieces[i]) - 1):
+                c0, c1 = pieces[i][h], pieces[i][h + 1]
+                raw[i, h] = sbuf("raw%d_%d" % (i, h), [P, PACK, c1 - c0], F32)
+                nc.sync.dma_start(raw[i, h][:], rows[:, :, c0:c1])
 
         x_scale = sbuf("x_scale", [P, S], U8)
         x_code = sbuf("x_code", [P, S], U32)
@@ -76,9 +78,9 @@ def tile_picked_maxout_max_po_kernel(
         def cast(copy, i, h, pairs):
             for u in pairs:
                 if h == 0:
-                    grouped[i, u] = sbuf("grouped%d_%d" % (i, u), [P, 2, P, PACK], BF16, tag="pair%d" % u)
+                    grouped[i, u] = sbuf("grouped%d_%d" % (i, u), [P, 2, P, PACK], BF16, tag=None if (i, u) == (2, 0) else "pair%d" % u)
                 copy(
-                    grouped[i, u][:, :, 64 * h : 64 * h + 64, :].rearrange("p t m j -> p m j t"),
+                    grouped[i, u][:, :, pieces[i][h] // PACK : pieces[i][h + 1] // PACK, :].rearrange("p t m j -> p m j t"),
                     raw[i, h][:].rearrange("p j (m t) -> p m j t", t=PACK)[:, :, :, 2 * u : 2 * u + 2],
                 )
 
@@ -117,37 +119,33 @@ def tile_picked_maxout_max_po_kernel(
         first = {}
         for u, h in by_pair:
             acc = product(0, u, h, 2 * u + h)
-            first[u, h] = sbuf("first%d_%d" % (u, h), [P, 2, HALF], F32)
-            nc.scalar.copy(first[u, h][:], acc[:])
+            if (u, h) != (1, 1):
+                first[u, h] = sbuf("first%d_%d" % (u, h), [P, 2, HALF], F32)
+                nc.scalar.copy(first[u, h][:], acc[:])
+        first_last = acc
+
+        def gpsimd_round(out, in_):
+            walk = "p m j t -> p m t j"
+            nc.gpsimd.tensor_scalar(out.rearrange(walk), in_.rearrange(walk), 1.0, 0.0, MULT, ADD)
 
         cast(nc.vector.tensor_copy, 1, 0, (0, 1))
         cast(nc.vector.tensor_copy, 1, 1, (0, 1))
         quantize(1, 0)
         quantize(1, 1)
-        cast(nc.vector.tensor_copy, 2, 0, (0,))
-        second = {}
-
-        def second_max(u, h, tag=None):
-            acc = product(1, u, h, 5 if (u, h) == (1, 1) else 4 + 2 * u + h)
-            second[u, h] = sbuf("second%d_%d" % (u, h), [P, 2, HALF], F32, tag=tag)
-            nc.vector.tensor_tensor(second[u, h][:], acc[:], first[u, h][:], MAX)
-
-        second_max(0, 0)
-        grouped[2, 1] = sbuf("grouped2_1", [P, 2, P, PACK], BF16, tag="first0_0")
-        nc.gpsimd.tensor_scalar(
-            grouped[2, 1][:, :, 0:64, :].rearrange("p t m j -> p m t j"),
-            raw[2, 0][:].rearrange("p j (m t) -> p m t j", t=PACK)[:, :, 2:4, :],
-            1.0,
-            0.0,
-            MULT,
-            ADD,
-        )
+        first[1, 1] = sbuf("first1_1", [P, 2, HALF], F32, tag="pair0")
+        nc.vector.tensor_copy(first[1, 1][:], first_last[:])
+        cast(nc.scalar.copy, 2, 0, (0,))
+        cast(gpsimd_round, 2, 0, (1,))
         cast(nc.scalar.copy, 2, 1, (0, 1))
+        cast(nc.scalar.copy, 2, 2, (0, 1))
         quantize(2, 0)
         quantize(2, 1)
-        second_max(0, 1)
-        second_max(1, 0)
-        second_max(1, 1, tag="raw2_1")
+        second = {}
+        for u, h in by_pair:
+            last = (u, h) == (1, 1)
+            acc = product(1, u, h, 5 if last else 4 + 2 * u + h)
+            second[u, h] = sbuf("second%d_%d" % (u, h), [P, 2, HALF], F32, tag="raw2_2" if last else None)
+            nc.vector.tensor_tensor(second[u, h][:], acc[:], first[u, h][:], MAX)
 
         y = [sbuf("y%d" % h, [P, PACK, HALF], F32) for h in range(2)]
         y_rows = out_0.rearrange("(p t) n -> p t n", t=PACK)

@@ -60,17 +60,6 @@ def tile_picked_maxout_max_po_kernel(
         nc.vector.tensor_copy(x_code[:], word_table[:].bitcast(U32).indirect(offsets[:]))
         nc.vector.tensor_copy(x_scale[:], scale_table[:].indirect(offsets[:]))
 
-        warm = psum.tile([P, S], F32, name="warm", tag="bank7")
-        nc.tensor.matmul_mx(
-            out=warm[:],
-            lhsT=x_code[:, 0:P].bitcast(FP8X4),
-            lhsT_scale=x_scale[:, 0:P],
-            rhs=x_code[:].bitcast(FP8X4),
-            rhs_scale=x_scale[:],
-            start=True,
-            stop=True,
-        )
-
         grouped = {}
         w_code = {}
         w_scale = {}

@@ -15,6 +15,9 @@ FP8X4 = mybir.dt.float8_e4m3fn_x4
 MAX = mybir.AluOpType.max
 MULT = mybir.AluOpType.mult
 ADD = mybir.AluOpType.add
+SUBTRACT = mybir.AluOpType.subtract
+COPY = mybir.ActivationFunctionType.Copy
+RELU = mybir.ActivationFunctionType.Relu
 
 P = 128
 PACK = 4
@@ -64,17 +67,18 @@ def tile_picked_maxout_max_po_kernel(
         w_code = {}
         w_scale = {}
 
-        def cast(copy, i, h, pairs):
-            for u in pairs:
-                if h == 0:
-                    grouped[i, u] = sbuf("grouped%d_%d" % (i, u), [P, 2, P, PACK], BF16, tag=None if (i, u) == (2, 0) else "pair%d" % u)
-                copy(
-                    grouped[i, u][:, :, pieces[i][h] // PACK : pieces[i][h + 1] // PACK, :].rearrange("p t m j -> p m j t"),
-                    raw[i, h][:].rearrange("p j (m t) -> p m j t", t=PACK)[:, :, :, 2 * u : 2 * u + 2],
-                )
+        slots = {(1, 0): "grouped0_0", (1, 1): "grouped0_1", (2, 1): "grouped0_1"}
 
-        def quantize(i, u):
-            w_code[i, u] = sbuf("w_code%d_%d" % (i, u), [P, 2 * P], U32)
+        def cast(copy, i, h, u):
+            if h == 0:
+                grouped[i, u] = sbuf("grouped%d_%d" % (i, u), [P, 2, P, PACK], BF16, tag=slots.get((i, u)))
+            copy(
+                grouped[i, u][:, :, pieces[i][h] // PACK : pieces[i][h + 1] // PACK, :].rearrange("p t m j -> p m j t"),
+                raw[i, h][:].rearrange("p j (m t) -> p m j t", t=PACK)[:, :, :, 2 * u : 2 * u + 2],
+            )
+
+        def quantize(i, u, tag=None):
+            w_code[i, u] = sbuf("w_code%d_%d" % (i, u), [P, 2 * P], U32, tag=tag)
             w_scale[i, u] = sbuf("w_scale%d_%d" % (i, u), [P, 2 * P], U8)
             nc.vector.quantize_mx(
                 out=w_code[i, u][:].bitcast(FP8X4),
@@ -82,59 +86,84 @@ def tile_picked_maxout_max_po_kernel(
                 in_=grouped[i, u][:].rearrange("p t m j -> p (t m j)"),
             )
 
-        def product(i, u, h, bank):
-            acc = psum.tile([P, 2, HALF], F32, name="acc%d_%d_%d" % (i, u, h), tag="bank%d" % bank)
+        def product(weights, u, h, bank):
+            acc = psum.tile(
+                [P, 2, HALF], F32, name="acc%d_%d_%d_%d" % (weights[0], len(weights), u, h), tag="bank%d" % bank
+            )
             cols = slice(h * HALF, (h + 1) * HALF)
             for e in range(2):
                 rows_e = slice(e * P, (e + 1) * P)
-                nc.tensor.matmul_mx(
-                    out=acc[:, e, :],
-                    lhsT=w_code[i, u][:, rows_e].bitcast(FP8X4),
-                    lhsT_scale=w_scale[i, u][:, rows_e],
-                    rhs=x_code[:, cols].bitcast(FP8X4),
-                    rhs_scale=x_scale[:, cols],
-                    start=True,
-                    stop=True,
-                )
+                for i in weights:
+                    nc.tensor.matmul_mx(
+                        out=acc[:, e, :],
+                        lhsT=w_code[i, u][:, rows_e].bitcast(FP8X4),
+                        lhsT_scale=w_scale[i, u][:, rows_e],
+                        rhs=x_code[:, cols].bitcast(FP8X4),
+                        rhs_scale=x_scale[:, cols],
+                        start=i == weights[0],
+                        stop=i == weights[-1],
+                    )
             return acc
 
-        by_pair = [(u, h) for u in range(2) for h in range(2)]
-        by_half = [(u, h) for h in range(2) for u in range(2)]
+        def scalar_negate(out, in_):
+            nc.scalar.activation(out, in_, COPY, scale=-1.0)
 
-        cast(nc.scalar.copy, 0, 0, (0, 1))
-        cast(nc.vector.tensor_copy, 0, 1, (0, 1))
-        quantize(0, 0)
-        quantize(0, 1)
-        first = {}
-        for u, h in by_pair:
-            acc = product(0, u, h, 2 * u + h)
-            if (u, h) != (1, 1):
-                first[u, h] = sbuf("first%d_%d" % (u, h), [P, 2, HALF], F32)
-                nc.scalar.copy(first[u, h][:], acc[:])
-        first_last = acc
+        def vector_negate(out, in_):
+            nc.vector.tensor_scalar_mul(out, in_, -1.0)
 
         def gpsimd_round(out, in_):
             walk = "p m j t -> p m t j"
             nc.gpsimd.tensor_scalar(out.rearrange(walk), in_.rearrange(walk), 1.0, 0.0, MULT, ADD)
 
-        cast(nc.vector.tensor_copy, 1, 0, (0, 1))
-        cast(nc.vector.tensor_copy, 1, 1, (0, 1))
+        by_half = [(u, h) for h in range(2) for u in range(2)]
+
+        cast(nc.scalar.copy, 0, 0, 0)
+        cast(scalar_negate, 0, 0, 1)
+        cast(nc.vector.tensor_copy, 0, 1, 0)
+        cast(vector_negate, 0, 1, 1)
+        quantize(0, 0)
+        quantize(0, 1)
+        held = {(u, h): product((0,), u, h, 2 * h + u) for u, h in by_half}
+        first = {}
+        for u, copy in enumerate((nc.scalar.copy, scalar_negate)):
+            first[u, 0] = sbuf("first%d_0" % u, [P, 2, HALF], F32)
+            copy(first[u, 0][:], held[u, 0][:])
+        negated = sbuf("negated", [P, 2, HALF], F32)
+        nc.scalar.copy(negated[:], held[1, 1][:])
+
+        for h in range(2):
+            for u in range(2):
+                cast(nc.vector.tensor_copy, 1, h, u)
         quantize(1, 0)
         quantize(1, 1)
-        first[1, 1] = sbuf("first1_1", [P, 2, HALF], F32, tag="pair0")
-        nc.vector.tensor_copy(first[1, 1][:], first_last[:])
-        cast(nc.scalar.copy, 2, 0, (0,))
-        cast(gpsimd_round, 2, 0, (1,))
-        cast(nc.scalar.copy, 2, 1, (0, 1))
-        cast(nc.scalar.copy, 2, 2, (0, 1))
-        quantize(2, 0)
-        quantize(2, 1)
+        first[0, 1] = sbuf("first0_1", [P, 2, HALF], F32, tag="grouped0_0")
+        nc.vector.tensor_copy(first[0, 1][:], held[0, 1][:])
+        cast(nc.scalar.copy, 2, 0, 0)
+        cast(gpsimd_round, 2, 0, 1)
+        for h in (1, 2):
+            for u in range(2):
+                cast(nc.scalar.copy, 2, h, u)
+
         second = {}
-        for u, h in by_pair:
-            last = (u, h) == (1, 1)
-            acc = product(1, u, h, 5 if last else 4 + 2 * u + h)
-            second[u, h] = sbuf("second%d_%d" % (u, h), [P, 2, HALF], F32, tag="raw2_2" if last else None)
+
+        def second_stage(u, h, acc):
+            second[u, h] = sbuf("second%d_%d" % (u, h), [P, 2, HALF], F32)
             nc.vector.tensor_tensor(second[u, h][:], acc[:], first[u, h][:], MAX)
+
+        for u in range(2):
+            second_stage(u, 0, product((1,), u, 0, 4 + u))
+        shared = product((1,), 0, 1, 6)
+        difference = product((1, 0), 1, 1, 7)
+        second[0, 1] = sbuf("second0_1", [P, 2, HALF], F32)
+        nc.vector.tensor_tensor(second[0, 1][:, 0, :], shared[:, 0, :], first[0, 1][:, 0, :], MAX)
+        quantize(2, 0, "first1_0")
+        quantize(2, 1, "first0_0")
+        nc.vector.tensor_tensor(second[0, 1][:, 1, :], shared[:, 1, :], first[0, 1][:, 1, :], MAX)
+
+        excess = sbuf("excess", [P, 2, HALF], F32, tag="raw2_2")
+        second[1, 1] = sbuf("second1_1", [P, 2, HALF], F32, tag="grouped0_1")
+        nc.scalar.activation(excess[:], difference[:], RELU)
+        nc.gpsimd.tensor_tensor(second[1, 1][:], excess[:], negated[:], SUBTRACT)
 
         y = [sbuf("y%d" % h, [P, PACK, HALF], F32) for h in range(2)]
         y_rows = out_0.rearrange("(p t) n -> p t n", t=PACK)
@@ -158,7 +187,7 @@ def tile_picked_maxout_max_po_kernel(
             )
 
         for u, h in by_half:
-            acc = product(2, u, h, 2 * u + h)
+            acc = product((2,), u, h, (0, 1, 2, 4)[2 * h + u])
             nc.vector.tensor_tensor(y[h][:, 2 * u : 2 * u + 2, :], acc[:], second[u, h][:], MAX)
             nc.sync.dma_start(
                 y_rows[:, 2 * u : 2 * u + 2, h * HALF : (h + 1) * HALF], y[h][:, 2 * u : 2 * u + 2, :]

@@ -140,9 +140,10 @@ def tile_picked_maxout_max_po_kernel(
         nc.vector.tensor_copy(first[0, 1][:], held[0, 1][:])
         cast(nc.scalar.copy, 2, 0, 0)
         cast(gpsimd_round, 2, 0, 1)
-        for h in (1, 2):
-            for u in range(2):
-                cast(nc.scalar.copy, 2, h, u)
+        cast(nc.scalar.copy, 2, 1, 0)
+        cast(gpsimd_round, 2, 1, 1)
+        for u in range(2):
+            cast(nc.scalar.copy, 2, 2, u)
 
         second = {}
 

from contextlib import ExitStack

import concourse.mybir as mybir

K, T, S, N = 512, 1024, 512, 512
FLOPS = 3 * 2 * K * S * N

F32 = mybir.dt.float32
BF16 = mybir.dt.bfloat16
I32 = mybir.dt.int32
U32 = mybir.dt.uint32
U16 = mybir.dt.uint16
U8 = mybir.dt.uint8
FP8X4 = mybir.dt.float8_e4m3fn_x4
MAX = mybir.AluOpType.max
MULT = mybir.AluOpType.mult
ADD = mybir.AluOpType.add
SUBTRACT = mybir.AluOpType.subtract
COPY = mybir.ActivationFunctionType.Copy
RELU = mybir.ActivationFunctionType.Relu

P = 128
PACK = 4
HALF = 256


def tile_picked_maxout_max_po_kernel(
    tc, x_words, x_scales, w1, w2, w3, offs, out_0, out_1, out_2
):
    nc = tc.nc
    with ExitStack() as ctx:
        sb = ctx.enter_context(tc.tile_pool(name="sb", bufs=1))
        psum = ctx.enter_context(tc.psum_pool(name="psum", bufs=1))

        def sbuf(name, shape, dtype, tag=None):
            return sb.tile(shape, dtype, name=name, tag=tag or name, align_bytes=64)

        offsets = sb.tile([P, S // 16], U16, name="offsets")

        scale_table = sbuf("scale_table", [P, T], U8)
        nc.vector.memset(scale_table[:].bitcast(I32), 0)
        word_table = sbuf("word_table", [P, T], I32)
        nc.sync.dma_start(word_table[:], x_words[0].rearrange("p n t -> p (n t)").bitcast(I32))
        nc.sync.dma_start(offsets[:], offs)
        for q in range(4):
            queue = nc.scalar if q < 2 else nc.sync
            queue.dma_start(
                scale_table[q:P:32, :].bitcast(I32),
                x_scales[0, q:16:4, :].bitcast(I32),
            )

        pieces = ((0, 256, 512), (0, 256, 512), (0, 256, 384, 512))
        raw = {}
        for i, w in enumerate((w1, w2, w3)):
            rows = w.rearrange("(p j) c -> p j c", j=PACK)
            for h in range(len(pieces[i]) - 1):
                c0, c1 = pieces[i][h], pieces[i][h + 1]
                raw[i, h] = sbuf("raw%d_%d" % (i, h), [P, PACK, c1 - c0], F32)
                nc.sync.dma_start(raw[i, h][:], rows[:, :, c0:c1])

        x_scale = sbuf("x_scale", [P, S], U8)
        x_code = sbuf("x_code", [P, S], U32)
        nc.vector.tensor_copy(x_code[:], word_table[:].bitcast(U32).indirect(offsets[:]))
        nc.vector.tensor_copy(x_scale[:], scale_table[:].indirect(offsets[:]))

        grouped = {}
        w_code = {}
        w_scale = {}

        slots = {(1, 0): "grouped0_0", (1, 1): "grouped0_1", (2, 1): "grouped0_1"}

        def cast(copy, i, h, u):
            if h == 0:
                grouped[i, u] = sbuf("grouped%d_%d" % (i, u), [P, 2, P, PACK], BF16, tag=slots.get((i, u)))
            copy(
                grouped[i, u][:, :, pieces[i][h] // PACK : pieces[i][h + 1] // PACK, :].rearrange("p t m j -> p m j t"),
                raw[i, h][:].rearrange("p j (m t) -> p m j t", t=PACK)[:, :, :, 2 * u : 2 * u + 2],
            )

        def quantize(i, u, tag=None):
            w_code[i, u] = sbuf("w_code%d_%d" % (i, u), [P, 2 * P], U32, tag=tag)
            w_scale[i, u] = sbuf("w_scale%d_%d" % (i, u), [P, 2 * P], U8)
            nc.vector.quantize_mx(
                out=w_code[i, u][:].bitcast(FP8X4),
                scales=w_scale[i, u][:],
                in_=grouped[i, u][:].rearrange("p t m j -> p (t m j)"),
            )

        def product(weights, u, h, bank):
            acc = psum.tile(
                [P, 2, HALF], F32, name="acc%d_%d_%d_%d" % (weights[0], len(weights), u, h), tag="bank%d" % bank
            )
            cols = slice(h * HALF, (h + 1) * HALF)
            for e in range(2):
                rows_e = slice(e * P, (e + 1) * P)
                for i in weights:
                    nc.tensor.matmul_mx(
                        out=acc[:, e, :],
                        lhsT=w_code[i, u][:, rows_e].bitcast(FP8X4),
                        lhsT_scale=w_scale[i, u][:, rows_e],
                        rhs=x_code[:, cols].bitcast(FP8X4),
                        rhs_scale=x_scale[:, cols],
                        start=i == weights[0],
                        stop=i == weights[-1],
                    )
            return acc

        def scalar_negate(out, in_):
            nc.scalar.activation(out, in_, COPY, scale=-1.0)

        def vector_negate(out, in_):
            nc.vector.tensor_scalar_mul(out, in_, -1.0)

        def gpsimd_round(out, in_):
            walk = "p m j t -> p m t j"
            nc.gpsimd.tensor_scalar(out.rearrange(walk), in_.rearrange(walk), 1.0, 0.0, MULT, ADD)

        by_half = [(u, h) for h in range(2) for u in range(2)]

        cast(nc.scalar.copy, 0, 0, 0)
        cast(scalar_negate, 0, 0, 1)
        cast(nc.vector.tensor_copy, 0, 1, 0)
        cast(vector_negate, 0, 1, 1)
        quantize(0, 0)
        quantize(0, 1)
        held = {(u, h): product((0,), u, h, 2 * h + u) for u, h in by_half}
        first = {}
        for u, copy in enumerate((nc.scalar.copy, scalar_negate)):
            first[u, 0] = sbuf("first%d_0" % u, [P, 2, HALF], F32)
            copy(first[u, 0][:], held[u, 0][:])
        negated = sbuf("negated", [P, 2, HALF], F32)
        nc.scalar.copy(negated[:], held[1, 1][:])

        for h in range(2):
            for u in range(2):
                cast(nc.vector.tensor_copy, 1, h, u)
        quantize(1, 0)
        quantize(1, 1)
        first[0, 1] = sbuf("first0_1", [P, 2, HALF], F32, tag="grouped0_0")
        nc.vector.tensor_copy(first[0, 1][:], held[0, 1][:])
        cast(nc.scalar.copy, 2, 0, 0)
        cast(gpsimd_round, 2, 0, 1)
        cast(nc.scalar.copy, 2, 1, 0)
        cast(gpsimd_round, 2, 1, 1)
        for u in range(2):
            cast(nc.scalar.copy, 2, 2, u)

        second = {}

        def second_stage(u, h, acc):
            second[u, h] = sbuf("second%d_%d" % (u, h), [P, 2, HALF], F32)
            nc.vector.tensor_tensor(second[u, h][:], acc[:], first[u, h][:], MAX)

        for u in range(2):
            second_stage(u, 0, product((1,), u, 0, 4 + u))
        shared = product((1,), 0, 1, 6)
        difference = product((1, 0), 1, 1, 7)
        second[0, 1] = sbuf("second0_1", [P, 2, HALF], F32)
        nc.vector.tensor_tensor(second[0, 1][:, 0, :], shared[:, 0, :], first[0, 1][:, 0, :], MAX)
        quantize(2, 0, "first1_0")
        quantize(2, 1, "first0_0")
        nc.vector.tensor_tensor(second[0, 1][:, 1, :], shared[:, 1, :], first[0, 1][:, 1, :], MAX)

        excess = sbuf("excess", [P, 2, HALF], F32, tag="raw2_2")
        second[1, 1] = sbuf("second1_1", [P, 2, HALF], F32, tag="grouped0_1")
        nc.scalar.activation(excess[:], difference[:], RELU)
        nc.gpsimd.tensor_tensor(second[1, 1][:], excess[:], negated[:], SUBTRACT)

        y = [sbuf("y%d" % h, [P, PACK, HALF], F32) for h in range(2)]
        y_rows = out_0.rearrange("(p t) n -> p t n", t=PACK)
        y_code = sbuf("y_code", [P, S], U32)
        y_scale = sbuf("y_scale", [P, S], U8)
        code_rows = out_1[0].rearrange("p n t -> p (n t)").bitcast(I32)

        def round_y(copy, name, h, c0, c1):
            g = sbuf(name, [P, c1 - c0, PACK], BF16)
            copy(
                g[:].rearrange("p (c i) t -> p c t i", i=4),
                y[h][:, :, c0:c1].rearrange("p t (c i) -> p c t i", i=4),
            )
            return g

        def quantize_y(g, c0, c1):
            nc.vector.quantize_mx(
                out=y_code[:, c0:c1].bitcast(FP8X4),
                scales=y_scale[:, c0:c1],
                in_=g[:].rearrange("p n t -> p (n t)"),
            )

        for u, h in by_half:
            acc = product((2,), u, h, (0, 1, 2, 4)[2 * h + u])
            nc.vector.tensor_tensor(y[h][:, 2 * u : 2 * u + 2, :], acc[:], second[u, h][:], MAX)
            nc.sync.dma_start(
                y_rows[:, 2 * u : 2 * u + 2, h * HALF : (h + 1) * HALF], y[h][:, 2 * u : 2 * u + 2, :]
            )
            if (u, h) == (1, 0):
                g0 = round_y(nc.scalar.copy, "y_round0", 0, 0, HALF)

        g2 = round_y(nc.scalar.copy, "y_round2", 1, P, HALF)
        g1 = round_y(nc.vector.tensor_copy, "y_round1", 1, 0, P)
        quantize_y(g0, 0, HALF)
        nc.sync.dma_start(code_rows[:, 0:HALF], y_code[:, 0:HALF].bitcast(I32))
        quantize_y(g1, HALF, HALF + P)
        quantize_y(g2, HALF + P, S)
        nc.sync.dma_start(code_rows[:, HALF:S], y_code[:, HALF:S].bitcast(I32))
        for q in range(4):
            queue = nc.scalar if q < 2 else nc.sync
            queue.dma_start(
                out_2[0, q:16:4, :].bitcast(I32),
                y_scale[q:P:32, :].bitcast(I32),
            )
